import numpy as np
import ml_dtypes


def mxq(x, axis, fmt="e4m3"):
    dtype, down = {"e4m3": (ml_dtypes.float8_e4m3fn, 7), "e5m2": (ml_dtypes.float8_e5m2, 14)}[fmt]
    v = np.moveaxis(np.asarray(x, np.float32).astype(ml_dtypes.bfloat16).astype(np.float64), axis, -1)
    blocks = v.reshape(v.shape[:-1] + (-1, 32))
    amax = np.abs(blocks).max(-1, keepdims=True)
    byte = np.maximum(np.where(amax > 0, np.frexp(amax)[1] - 1 + 127, 0) - down, 1)
    scale = np.exp2(byte - 127.0)
    codes = (blocks / scale).astype(np.float32).astype(dtype).astype(np.float64)
    return np.moveaxis((codes * scale).reshape(v.shape), -1, axis)


WIDE = False


def mx_kscale(k):
    if not WIDE:
        return np.ones(k)
    levels = np.array([10, -10, 5, -5, 0])
    if k % 512:
        return np.exp2(np.random.permutation(np.resize(levels, k // 32))).repeat(32)
    a = np.empty((k // 512, 16))
    for p in range(k // 512):
        a[p, :8] = np.random.permutation(np.resize(levels, 8))
        for g in range(8):
            far = levels[np.abs(levels - a[p, g]) >= 10]
            a[p, g + 8] = far[np.random.randint(len(far))]
    return np.exp2(a.ravel()).repeat(32)


BF16 = ml_dtypes.bfloat16


def bf(x):
    return np.asarray(x, np.float32).astype(BF16)


def f64(x):
    return np.asarray(x).astype(np.float64)


E2M1 = np.array([0.0, 0.5, 1.0, 1.5, 2.0, 3.0, 4.0, 6.0, -0.0, -0.5, -1.0, -1.5, -2.0, -3.0, -4.0, -6.0])


def pack_weight(w, fmt):
    k, n = w.shape
    w = f64(bf(w)).reshape(k // 32, 32, n)
    amax = np.abs(w).max(1)
    if fmt == "e4m3":
        byte = np.frexp(amax)[1] - 1 + 127 - 7
    else:
        mant, ex = np.frexp(amax / 6.0)
        byte = np.where(mant > 0.5, ex, ex - 1) + 127
    byte = np.clip(np.where(amax > 0, byte, 1), 1, 254)
    scaled = (w * np.exp2(127.0 - byte)[:, None, :]).reshape(k, n).astype(np.float32)
    by_word = np.ascontiguousarray(scaled.reshape(k // 512, 128, 4, n).transpose(0, 1, 3, 2))
    if fmt == "e4m3":
        words = by_word.astype(ml_dtypes.float8_e4m3fn).view(np.uint8)
    else:
        c = by_word.astype(ml_dtypes.float4_e2m1fn).view(np.uint8) & 0xF
        words = c[..., 0::2] | (c[..., 1::2] << 4)
    return np.ascontiguousarray(words), np.ascontiguousarray(byte.astype(np.uint8).reshape(k // 512, 16, n))


def unpack_weight(words, scales, fmt):
    g, p, n, _ = words.shape
    if fmt == "e4m3":
        vals = np.ascontiguousarray(words).view(ml_dtypes.float8_e4m3fn).astype(np.float64)
    else:
        nib = np.empty((g, p, n, 4), np.uint8)
        nib[..., 0::2] = words & 0xF
        nib[..., 1::2] = words >> 4
        vals = E2M1[nib]
    vals = vals * np.repeat(np.exp2(scales.astype(np.float64) - 127.0), 8, axis=1)[..., None]
    return vals.transpose(0, 1, 3, 2).reshape(g * 512, n)
def pack4(w):
    words, scales = pack_weight(w, "e2m1")
    return words.reshape(words.shape[0], 128, -1), scales


def unpack4(words, scales):
    return unpack_weight(words.reshape(words.shape[0], 128, -1, 2), scales, "e2m1")


def planes(Y):
    n, m = Y.shape
    b = f64(bf(Y)).reshape(n // 32, 32, m)
    amax = np.abs(b).max(1)
    byte = np.clip(np.where(amax > 0, np.frexp(amax)[1] - 1 + 127 - 7, 1), 1, 254)
    codes = (b * np.exp2(127.0 - byte)[:, None, :]).reshape(n, m).astype(np.float32).astype(ml_dtypes.float8_e4m3fn).view(np.uint8)
    words = codes.reshape(n // 512, 128, 4, m).transpose(0, 1, 3, 2)
    return np.ascontiguousarray(words), np.ascontiguousarray(byte.astype(np.uint8).reshape(n // 512, 16, m))


G, T, K, F, D = 4, 512, 512, 1024, 1024
BANDWIDTH = 16.0

def setup_inputs():
    s, t = mx_kscale(K), mx_kscale(F)
    level = np.random.uniform(-0.5, 0.5, T)
    freq = 2 * np.pi * BANDWIDTH * np.random.randn(K // 2)
    phase = level[:, None] * freq[None, :]
    feats = np.sqrt(2) * np.concatenate([np.sin(phase), np.cos(phase)], axis=1)
    w1 = np.random.randn(G * K, F) / np.sqrt(K) / np.tile(s, G)[:, None]
    spread = np.exp(0.8 * np.random.randn(G, D))
    w2 = 2 * np.random.randn(G, F, D) / np.sqrt(F) * spread[:, None, :] / t[None, :, None]
    w1_words, w1_scales = pack4(w1)
    w2_words, w2_scales = pack4(w2.reshape(G * F, D))
    return {
        "feats": bf(feats * s[None, :]),
        "w1_words": w1_words, "w1_scales": w1_scales,
        "b1": bf(0.3 * np.random.randn(G, F)),
        "gain": bf((1 + 0.1 * np.random.randn(G, F)) * t[None, :]),
        "w2_words": w2_words, "w2_scales": w2_scales,
        "fade": bf(1 / np.sqrt(1 + np.exp(8 * level))),
        "table": bf(0.5 * np.random.randn(G, D) * spread),
    }

def reference(feats, w1_words, w1_scales, b1, gain, w2_words, w2_scales, fade, table):
    e = mxq(f64(feats), 1)
    w1 = unpack4(w1_words, w1_scales).reshape(G, K, F)
    z = (e @ w1) + f64(b1)[:, None, :]
    h = z / (1 + np.exp(-z)) * f64(gain)[:, None, :]
    w2 = unpack4(w2_words, w2_scales).reshape(G, F, D)
    p = mxq(h, 2) @ w2
    y = p * f64(fade)[None, :, None] + f64(table)[:, None, :]
    Y = y.transpose(2, 0, 1).reshape(D, G * T)
    words, scales = planes(Y)
    return y, words, scales

@@ -1,0 +1,322 @@
+from contextlib import ExitStack
+
+import concourse.mybir as mybir
+from concourse.masks import make_identity
+
+G, T, K, F, D = 4, 512, 512, 1024, 1024
+FLOPS = 2 * G * T * (K * F + F * D)
+
+F32 = mybir.dt.float32
+BF16 = mybir.dt.bfloat16
+I32 = mybir.dt.int32
+U32 = mybir.dt.uint32
+U8 = mybir.dt.uint8
+FP8X4 = mybir.dt.float8_e4m3fn_x4
+FP4X4 = mybir.dt.float4_e2m1fn_x4
+ACT = mybir.ActivationFunctionType
+ALU = mybir.AluOpType
+
+P = 128
+HALVES = 2 * G
+SILU_LEAD = 3
+ORDER = """mm1:0,0 silu:0,0 mm1:0,1 silu:0,1 mm1:0,2 silu:0,2 mm1:0,3 silu:0,3 mm1:1,0 mm1:1,1 gain:0 silu:1,0
+mm1:1,2 silu:1,1 mm1:1,3 silu:1,2 mm1:2,0 silu:1,3 mm1:2,1 pc:6 qh:0 gain:1 silu:2,0 mm1:2,2
+silu:2,1 mm1:2,3 silu:2,2 mm1:3,0 silu:2,3 mm1:3,1 pc:7 qh:1 mm2:0,0 mm2:0,1 gain:2 silu:3,0 mm1:3,2
+silu:3,1 mm1:3,3 mm2:0,2 mm2:0,3 silu:3,2 mm1:4,0 silu:3,3 mm1:4,1 stt:0,0 qh:2 cast:0,0 mm2:1,0
+stt:0,1 cast:0,1 mm2:1,1 tr:0,0 sty:0,0 stt:0,2 cast:0,2 stt:0,3 cast:0,3 sty:0,1 gain:3 silu:4,0
+tr:0,1 mm1:4,2 silu:4,1 mm1:4,3 mm2:1,2 mm2:1,3 wc:0,0 silu:4,2 mm1:5,0 wc:0,1 silu:4,3 mm1:5,1
+stt:1,0 qh:3 cast:1,0 mm2:2,0 stt:1,1 cast:1,1 mm2:2,1 tr:1,0 sty:1,0 stt:1,2 cast:1,2 stt:1,3
+cast:1,3 sty:1,1 qy:0 gain:4 silu:5,0 tr:1,1 mm1:5,2 silu:5,1 mm1:5,3 mm2:2,2 mm2:2,3 wc:1,0
+silu:5,2 mm1:6,0 wc:1,1 silu:5,3 mm1:6,1 stt:2,0 qh:4 cast:2,0 mm2:3,0 stt:2,1 cast:2,1 mm2:3,1
+tr:2,0 sty:2,0 stt:2,2 cast:2,2 stt:2,3 cast:2,3 sty:2,1 qy:1 gain:5 silu:6,0 tr:2,1 mm1:6,2
+silu:6,1 mm1:6,3 mm2:3,2 mm2:3,3 wc:2,0 silu:6,2 mm1:7,0 wc:2,1 silu:6,3 mm1:7,1 stt:3,0 qh:5
+cast:3,0 mm2:4,0 stt:3,1 cast:3,1 mm2:4,1 tr:3,0 sty:3,0 stt:3,2 cast:3,2 stt:3,3 cast:3,3 sty:3,1
+qy:2 gain:6 silu:7,0 tr:3,1 mm1:7,2 silu:7,1 mm1:7,3 mm2:4,2 mm2:4,3 wc:3,0 silu:7,2 wc:3,1 silu:7,3
+stt:4,0 qh:6 cast:4,0 mm2:5,0 stt:4,1 cast:4,1 mm2:5,1 tr:4,0 sty:4,0 stt:4,2 cast:4,2 stt:4,3
+cast:4,3 sty:4,1 qy:3 gain:7 tr:4,1 mm2:5,2 mm2:5,3 wc:4,0 wc:4,1 stt:5,0 qh:7 cast:5,0 mm2:6,0
+stt:5,1 cast:5,1 mm2:6,1 tr:5,0 sty:5,0 stt:5,2 cast:5,2 stt:5,3 cast:5,3 sty:5,1 qy:4 tr:5,1
+mm2:6,2 mm2:6,3 wc:5,0 wc:5,1 stt:6,0 mm2:7,0 cast:6,0 stt:6,1 mm2:7,1 cast:6,1 sty:6,0 stt:6,2
+mm2:7,2 cast:6,2 stt:6,3 mm2:7,3 tr:6,0 cast:6,3 sty:6,1 qy:5 ss:0,1536 tr:6,1 stt:7,0 wc:6,0
+stt:7,1 sty:7,0 cast:7,0 stt:7,2 cast:7,1 tr:7,0 stt:7,3 sty:7,1 wcv:6,1 cast:7,2 tri:7,2 castv:7,3
+tri:7,3 qy:6 wc:7,0 wciv:7,2 wci:7,3 qyh:7,0 qyh:7,1 sse:1536,2048
+"""
+
+
+def tile_noise_level_bias_table_k7_kernel(
+    tc, feats, w1_words, w1_scales, b1, gain, w2_words, w2_scales, fade, table, out_0, out_1, out_2
+):
+    nc = tc.nc
+    with ExitStack() as ctx:
+        keep = ctx.enter_context(tc.tile_pool(name="keep", bufs=1))
+        work = ctx.enter_context(tc.tile_pool(name="work", bufs=2))
+        psum = ctx.enter_context(tc.psum_pool(name="psum", bufs=2))
+        ctx.enter_context(tc.manual_schedule())
+
+        ident = keep.tile([P, P], F32)
+        vec_rows = keep.tile([P, 512], BF16)
+        vec = keep.tile([P, 2 * HALVES, 4], F32)
+        fade_col = keep.tile([P, 4, 2], BF16)
+        warm = keep.tile([P, 8], F32)
+        feats_rows = keep.tile([P, 4, K], BF16)
+        feats_k = keep.tile([P, T, 2], F32, align_bytes=64)
+        feats_q = keep.tile([P, T], U32, align_bytes=64)
+        feats_s = keep.tile([P, T], U8, align_bytes=64)
+        w1_raw0 = keep.tile([P, 1, 2 * F], U8, align_bytes=64)
+        w1_raw = keep.tile([P, G - 1, 2 * F], U8, align_bytes=64)
+        w1s_raw0 = keep.tile([P, 1, F], U8, align_bytes=64)
+        w1s_raw = keep.tile([P, G - 1, F], U8, align_bytes=64)
+        w1_q = keep.tile([P, HALVES, 1024], U8, align_bytes=64)
+        w1_s = keep.tile([P, G, F], U8, align_bytes=64)
+        w2_q = keep.tile([P, HALVES, 2 * D], U8, align_bytes=64)
+        w2_s = keep.tile([P, HALVES, D], U8, align_bytes=64)
+        table_all = keep.tile([P, G, D], BF16)
+        y_s = keep.tile([P, 2, G * T], U8, align_bytes=64)
+
+        def load_scale_rows(queue, plane, rows):
+            for quad in range(4):
+                queue.dma_start(
+                    out=plane[32 * quad : 32 * quad + 4].bitcast(I32),
+                    in_=rows[:, 4 * quad : 4 * quad + 4, :].rearrange("g r n -> r g n").bitcast(I32),
+                )
+
+        nc.vector.memset(vec_rows[:], 0.0)
+        nc.vector.memset(w1s_raw0[:].bitcast(I32), 0)
+        nc.vector.memset(warm[:], 0.0)
+        nc.vector.memset(w1s_raw[:].bitcast(I32), 0)
+        nc.vector.memset(w2_s[:].bitcast(I32), 0)
+        make_identity(nc, ident[:])
+
+        nc.sync.dma_start(out=vec_rows[0:HALVES, :], in_=b1.rearrange("b (g c) -> (b g) c", g=2))
+        nc.scalar.dma_start(
+            out=vec_rows[HALVES : 2 * HALVES, :], in_=gain.rearrange("b (g c) -> (b g) c", g=2)
+        )
+        nc.sync.dma_start(out=feats_rows[:], in_=feats.rearrange("(i q) k -> q i k", q=P))
+        nc.sync.dma_start(
+            out=w1_raw0[:].bitcast(I32), in_=w1_words[0:1].rearrange("g p n -> p g n").bitcast(I32)
+        )
+        load_scale_rows(nc.scalar, w1s_raw0, w1_scales[0:1])
+        nc.scalar.activation(out=warm[:, 4:5], in_=warm[:, 0:1], func=ACT.Silu)
+        load_scale_rows(nc.sync, w1s_raw, w1_scales[1:G])
+        nc.sync.dma_start(
+            out=w1_raw[:].bitcast(I32), in_=w1_words[1:G].rearrange("g p n -> p g n").bitcast(I32)
+        )
+        load_scale_rows(nc.sync, w2_s, w2_scales)
+        with nc.allow_non_contiguous_dma(reason="one fade value a partition"):
+            nc.sync.dma_start(
+                out=fade_col[:, :, 0:1], in_=fade.rearrange("(i q o) -> q i o", q=P, o=1)
+            )
+        for b in range(G):
+            nc.sync.dma_start(
+                out=w2_q[:, 2 * b : 2 * b + 2, :].bitcast(I32),
+                in_=w2_words[2 * b : 2 * b + 2].rearrange("g p n -> p g n").bitcast(I32),
+            )
+            nc.sync.dma_start(out=table_all[:, b, :], in_=table[b].partition_broadcast(P))
+
+        def turn_words(bank, slot, words):
+            nc.tensor.transpose(bank[:, slot * P : (slot + 1) * P], words, ident[:])
+
+        vec_bank = psum.tile([P, 512], F32, tag="z", name="vec_bank")
+        vec_words = vec_rows[:].bitcast(F32)
+        for u in range(2):
+            turn_words(vec_bank, u, vec_words[:, u:256:2])
+        nc.scalar.copy(
+            out=vec[:].rearrange("p r (u e) -> p r u e", e=2),
+            in_=vec_bank[:, 0 : 2 * P].bitcast(BF16).rearrange("p (u r e) -> p r u e", u=2, e=2)[
+                :, 0 : 2 * HALVES
+            ],
+        )
+
+        def order_w1_words(half):
+            b, g = divmod(half, 2)
+            raw = w1_raw0[:, 0, :] if b == 0 else w1_raw[:, b - 1, :]
+            nc.vector.tensor_copy(
+                out=w1_q[:, half, :].rearrange("p (t m e) -> p t m e", t=4, e=2),
+                in_=raw[:, 1024 * g : 1024 * (g + 1)].rearrange("p (m t e) -> p t m e", t=4, e=2),
+            )
+
+        def order_w1_scales(b):
+            raw = w1s_raw0[:, 0, :] if b == 0 else w1s_raw[:, b - 1, :]
+            nc.vector.tensor_copy(
+                out=w1_s[:, b, :].rearrange("p (g t m) -> p g t m", g=2, t=4),
+                in_=raw.rearrange("p (g m t) -> p g t m", g=2, t=4),
+            )
+
+        feats_words = feats_rows[:].bitcast(F32)
+        feats_banks = []
+        for pair in range(2):
+            bank = psum.tile([P, 512], F32, tag="t", name="feats_bank")
+            for j in range(2):
+                for u in range(2):
+                    turn_words(bank, 2 * j + u, feats_words[:, 2 * pair + j, u:256:2])
+            feats_banks.append(bank)
+        for pair in range(2):
+            nc.scalar.copy(
+                out=feats_k[:, 256 * pair : 256 * (pair + 1), :].rearrange("p (j q) u -> p j q u", j=2),
+                in_=feats_banks[pair][:].rearrange("p (j u q) -> p j q u", j=2, u=2),
+            )
+        order_w1_scales(0)
+        order_w1_words(0)
+        order_w1_words(1)
+        order_w1_scales(1)
+        order_w1_words(2)
+        order_w1_words(3)
+        nc.vector.quantize_mx(
+            out=feats_q[:].bitcast(FP8X4),
+            scales=feats_s[:],
+            in_=feats_k[:].rearrange("p n u -> p (n u)").bitcast(BF16),
+        )
+        order_w1_scales(2)
+        order_w1_words(4)
+        order_w1_words(5)
+        order_w1_scales(3)
+
+        z_banks, silu_tiles, h_tiles, h_q, h_s = {}, {}, {}, {}, {}
+        p_banks, y_tiles, yb_tiles, t_banks, yk_tiles = {}, {}, {}, {}, {}
+
+        def first_matmul(half, t):
+            b, g = divmod(half, 2)
+            bank = psum.tile([P, T], F32, tag="z", name="z_bank")
+            nc.tensor.matmul_mx(
+                out=bank[:],
+                lhsT=w1_q[:, half, 256 * t : 256 * (t + 1)].bitcast(FP4X4),
+                lhsT_scale=w1_s[:, b, 512 * g + P * t : 512 * g + P * (t + 1)],
+                rhs=feats_q[:].bitcast(FP8X4),
+                rhs_scale=feats_s[:],
+                start=True,
+                stop=True,
+            )
+            z_banks[half, t] = bank
+
+        def silu(half, t):
+            if t == 0:
+                silu_tiles[half] = work.tile([P, 4, T], F32, tag="silu", name="silu_tile", bufs=SILU_LEAD + 1)
+            nc.scalar.activation(
+                out=silu_tiles[half][:, t, :], in_=z_banks[half, t][:], func=ACT.Silu, bias=vec[:, half, t : t + 1]
+            )
+
+        def apply_gain(half):
+            h = work.tile([P, 4 * T], BF16, tag="h", name="h_tile", align_bytes=64)
+            nc.vector.tensor_tensor(
+                out=h[:].rearrange("p (j e t) -> p j t e", e=2, t=4),
+                in0=silu_tiles[half][:].rearrange("p t (j e) -> p j t e", e=2),
+                in1=vec[:, HALVES + half, :].unsqueeze(1).unsqueeze(3).to_broadcast([P, T // 2, 4, 2]),
+                op=ALU.mult,
+            )
+            h_tiles[half] = h
+
+        def quantize_h(half):
+            codes = work.tile([P, T], U32, tag="hq", name="h_codes", bufs=4, align_bytes=64)
+            scales = work.tile([P, T], U8, tag="hs", name="h_scales", bufs=4, align_bytes=64)
+            nc.vector.quantize_mx(out=codes[:].bitcast(FP8X4), scales=scales[:], in_=h_tiles[half][:])
+            h_q[half], h_s[half] = codes, scales
+
+        def second_matmul(half, i):
+            b, g = divmod(half, 2)
+            bank = psum.tile([P, 512], F32, tag="p", name="p_bank", bufs=4)
+            for kp in range(2):
+                nc.tensor.matmul_mx(
+                    out=bank[:],
+                    lhsT=h_q[2 * b + kp][:, P * i : P * (i + 1)].bitcast(FP8X4),
+                    lhsT_scale=h_s[2 * b + kp][:, P * i : P * (i + 1)],
+                    rhs=w2_q[:, 2 * b + kp, 1024 * g : 1024 * (g + 1)].bitcast(FP4X4),
+                    rhs_scale=w2_s[:, 2 * b + kp, 512 * g : 512 * (g + 1)],
+                    start=(kp == 0),
+                    stop=(kp == 1),
+                )
+            p_banks[half, i] = bank
+
+        def fade_and_table(half, i):
+            b, g = divmod(half, 2)
+            pair, j = divmod(i, 2)
+            if j == 0:
+                y_tiles[half, pair] = work.tile([P, 2, 512], F32, tag="y", name="y_tile", bufs=5)
+            nc.vector.scalar_tensor_tensor(
+                out=y_tiles[half, pair][:, j, :],
+                in0=p_banks[half, i][:],
+                scalar=fade_col[:, i, 0:1],
+                in1=table_all[:, b, 512 * g : 512 * (g + 1)],
+                op0=ALU.mult,
+                op1=ALU.add,
+            )
+
+        def store_y(half, pair):
+            b, g = divmod(half, 2)
+            nc.sync.dma_start(
+                out=out_0[b, 256 * pair : 256 * (pair + 1), 512 * g : 512 * (g + 1)].rearrange(
+                    "(j q) c -> q j c", q=P
+                ),
+                in_=y_tiles[half, pair][:],
+            )
+
+        def round_y(half, i, engine_copy):
+            pair, j = divmod(i, 2)
+            if j == 0:
+                yb_tiles[half, pair] = work.tile([P, 2, 512], BF16, tag="yb", name="yb_tile", bufs=4)
+            engine_copy(
+                out=yb_tiles[half, pair][:, j, :].rearrange("q (u p e) -> q u p e", u=2, e=2),
+                in_=y_tiles[half, pair][:, j, :].rearrange("q (p u e) -> q u p e", u=2, e=2),
+            )
+
+        def turn_y(half, first, count, tag="t", bufs=2):
+            bank = psum.tile([P, 512], F32, tag=tag, name="y_bank", bufs=bufs)
+            pair, j = divmod(first, 2)
+            words = yb_tiles[half, pair][:].rearrange("q j c -> q (j c)").bitcast(F32)
+            for slot in range(2 * count):
+                turn_words(bank, slot, words[:, P * (2 * j + slot) : P * (2 * j + slot + 1)])
+            t_banks[half, first] = bank
+
+        def gather_y(half, first, count, engine_copy):
+            if half not in yk_tiles:
+                yk_tiles[half] = work.tile([P, T, 2], F32, tag="yk", name="yk_tile", align_bytes=64)
+            engine_copy(
+                out=yk_tiles[half][:, P * first : P * (first + count), :].rearrange("p (j q) u -> p j q u", j=count),
+                in_=t_banks[half, first][:, 0 : 2 * P * count].rearrange("p (j u q) -> p j q u", j=count, u=2),
+            )
+
+        def quantize_y(half, first, count):
+            b, g = divmod(half, 2)
+            cols = slice(T * b + P * first, T * b + P * (first + count))
+            codes = work.tile([P, P * count], U32, tag="yq", name="y_codes", bufs=3, align_bytes=64)
+            nc.vector.quantize_mx(
+                out=codes[:].bitcast(FP8X4),
+                scales=y_s[:, g, cols],
+                in_=yk_tiles[half][:, P * first : P * (first + count), :].rearrange("p n u -> p (n u)").bitcast(BF16),
+            )
+            nc.sync.dma_start(
+                out=out_1[g].rearrange("p m t -> p (m t)")[:, 4 * cols.start : 4 * cols.stop].bitcast(I32),
+                in_=codes[:].bitcast(I32),
+            )
+
+        def store_y_scales(first, last, queues):
+            for quad in range(4):
+                queues[quad % len(queues)].dma_start(
+                    out=out_2[:, 4 * quad : 4 * quad + 4, first:last].rearrange("g r m -> r g m").bitcast(I32),
+                    in_=y_s[32 * quad : 32 * quad + 4, :, first:last].bitcast(I32),
+                )
+
+        on_scalar, on_vector = nc.scalar.copy, nc.vector.tensor_copy
+        calls = {
+            "mm1": first_matmul,
+            "silu": silu,
+            "gain": apply_gain,
+            "qh": quantize_h,
+            "pc": order_w1_words,
+            "mm2": second_matmul,
+            "stt": fade_and_table,
+            "sty": store_y,
+            "cast": lambda half, i: round_y(half, i, on_scalar),
+            "castv": lambda half, i: round_y(half, i, on_vector),
+            "tr": lambda half, pair: turn_y(half, 2 * pair, 2),
+            "tri": lambda half, i: turn_y(half, i, 1, "z", 2),
+            "wc": lambda half, pair: gather_y(half, 2 * pair, 2, on_scalar),
+            "wcv": lambda half, pair: gather_y(half, 2 * pair, 2, on_vector),
+            "wci": lambda half, i: gather_y(half, i, 1, on_scalar),
+            "wciv": lambda half, i: gather_y(half, i, 1, on_vector),
+            "qy": lambda half: quantize_y(half, 0, 4),
+            "qyh": lambda half, pair: quantize_y(half, 2 * pair, 2),
+            "ss": lambda first, last: store_y_scales(first, last, [nc.sync]),
+            "sse": lambda first, last: store_y_scales(first, last, [nc.scalar, nc.sync]),
+        }
+        for item in ORDER.split():
+            call, args = item.split(":")
+            calls[call](*[int(a) for a in args.split(",")])

@@ -20,25 +20,25 @@ P = 128
 HALVES = 2 * G
 SILU_LEAD = 3
 ORDER = """mm1:0,0 silu:0,0 mm1:0,1 silu:0,1 mm1:0,2 silu:0,2 mm1:0,3 silu:0,3 mm1:1,0 mm1:1,1 gain:0 silu:1,0
-mm1:1,2 silu:1,1 mm1:1,3 silu:1,2 mm1:2,0 silu:1,3 mm1:2,1 pc:6 qh:0 gain:1 silu:2,0 mm1:2,2
-silu:2,1 mm1:2,3 silu:2,2 mm1:3,0 silu:2,3 mm1:3,1 pc:7 qh:1 mm2:0,0 mm2:0,1 gain:2 silu:3,0 mm1:3,2
-silu:3,1 mm1:3,3 mm2:0,2 mm2:0,3 silu:3,2 mm1:4,0 silu:3,3 mm1:4,1 stt:0,0 qh:2 cast:0,0 mm2:1,0
-stt:0,1 cast:0,1 mm2:1,1 tr:0,0 sty:0,0 stt:0,2 cast:0,2 stt:0,3 cast:0,3 sty:0,1 gain:3 silu:4,0
-tr:0,1 mm1:4,2 silu:4,1 mm1:4,3 mm2:1,2 mm2:1,3 wc:0,0 silu:4,2 mm1:5,0 wc:0,1 silu:4,3 mm1:5,1
-stt:1,0 qh:3 cast:1,0 mm2:2,0 stt:1,1 cast:1,1 mm2:2,1 tr:1,0 sty:1,0 stt:1,2 cast:1,2 stt:1,3
-cast:1,3 sty:1,1 qy:0 gain:4 silu:5,0 tr:1,1 mm1:5,2 silu:5,1 mm1:5,3 mm2:2,2 mm2:2,3 wc:1,0
-silu:5,2 mm1:6,0 wc:1,1 silu:5,3 mm1:6,1 stt:2,0 qh:4 cast:2,0 mm2:3,0 stt:2,1 cast:2,1 mm2:3,1
-tr:2,0 sty:2,0 stt:2,2 cast:2,2 stt:2,3 cast:2,3 sty:2,1 qy:1 gain:5 silu:6,0 tr:2,1 mm1:6,2
-silu:6,1 mm1:6,3 mm2:3,2 mm2:3,3 wc:2,0 silu:6,2 mm1:7,0 wc:2,1 silu:6,3 mm1:7,1 stt:3,0 qh:5
-cast:3,0 mm2:4,0 stt:3,1 cast:3,1 mm2:4,1 tr:3,0 sty:3,0 stt:3,2 cast:3,2 stt:3,3 cast:3,3 sty:3,1
-qy:2 gain:6 silu:7,0 tr:3,1 mm1:7,2 silu:7,1 mm1:7,3 mm2:4,2 mm2:4,3 wc:3,0 silu:7,2 wc:3,1 silu:7,3
-stt:4,0 qh:6 cast:4,0 mm2:5,0 stt:4,1 cast:4,1 mm2:5,1 tr:4,0 sty:4,0 stt:4,2 cast:4,2 stt:4,3
-cast:4,3 sty:4,1 qy:3 gain:7 tr:4,1 mm2:5,2 mm2:5,3 wc:4,0 wc:4,1 stt:5,0 qh:7 cast:5,0 mm2:6,0
-stt:5,1 cast:5,1 mm2:6,1 tr:5,0 sty:5,0 stt:5,2 cast:5,2 stt:5,3 cast:5,3 sty:5,1 qy:4 tr:5,1
-mm2:6,2 mm2:6,3 wc:5,0 wc:5,1 stt:6,0 mm2:7,0 cast:6,0 stt:6,1 mm2:7,1 cast:6,1 sty:6,0 stt:6,2
-mm2:7,2 cast:6,2 stt:6,3 mm2:7,3 tr:6,0 cast:6,3 sty:6,1 qy:5 ss:0,1536 tr:6,1 stt:7,0 wc:6,0
-stt:7,1 sty:7,0 cast:7,0 stt:7,2 cast:7,1 tr:7,0 stt:7,3 sty:7,1 wcv:6,1 cast:7,2 tri:7,2 castv:7,3
-tri:7,3 qy:6 wc:7,0 wciv:7,2 wci:7,3 qyh:7,0 qyh:7,1 sse:1536,2048
+mm1:1,2 silu:1,1 mm1:1,3 rows:0 silu:1,2 mm1:2,0 silu:1,3 mm1:2,1 tb:0 pc:6 qh:0 gain:1 silu:2,0
+mm1:2,2 silu:2,1 mm1:2,3 tc:0 tb:1 silu:2,2 mm1:3,0 silu:2,3 mm1:3,1 tc:1 tb:2 tb:3 pc:7 qh:1
+mm2:0,0 mm2:0,1 gain:2 silu:3,0 mm1:3,2 silu:3,1 tc:2 tc:3 mm1:3,3 mm2:0,2 mm2:0,3 silu:3,2 mm1:4,0
+silu:3,3 mm1:4,1 stt:0,0 qh:2 cast:0,0 mm2:1,0 stt:0,1 cast:0,1 mm2:1,1 tr:0,0 sty:0,0 stt:0,2
+cast:0,2 stt:0,3 cast:0,3 sty:0,1 gain:3 silu:4,0 tr:0,1 mm1:4,2 silu:4,1 mm1:4,3 mm2:1,2 mm2:1,3
+wc:0,0 silu:4,2 mm1:5,0 wc:0,1 silu:4,3 mm1:5,1 stt:1,0 qh:3 cast:1,0 mm2:2,0 stt:1,1 cast:1,1
+mm2:2,1 tr:1,0 sty:1,0 stt:1,2 cast:1,2 stt:1,3 cast:1,3 sty:1,1 qy:0 gain:4 silu:5,0 tr:1,1 mm1:5,2
+silu:5,1 mm1:5,3 mm2:2,2 mm2:2,3 wc:1,0 silu:5,2 mm1:6,0 wc:1,1 silu:5,3 mm1:6,1 stt:2,0 qh:4
+cast:2,0 mm2:3,0 stt:2,1 cast:2,1 mm2:3,1 tr:2,0 sty:2,0 stt:2,2 cast:2,2 stt:2,3 cast:2,3 sty:2,1
+qy:1 gain:5 silu:6,0 tr:2,1 mm1:6,2 silu:6,1 mm1:6,3 mm2:3,2 mm2:3,3 wc:2,0 silu:6,2 mm1:7,0 wc:2,1
+silu:6,3 mm1:7,1 stt:3,0 qh:5 cast:3,0 mm2:4,0 stt:3,1 cast:3,1 mm2:4,1 tr:3,0 sty:3,0 stt:3,2
+cast:3,2 stt:3,3 cast:3,3 sty:3,1 qy:2 gain:6 silu:7,0 tr:3,1 mm1:7,2 silu:7,1 mm1:7,3 mm2:4,2
+mm2:4,3 wc:3,0 silu:7,2 wc:3,1 silu:7,3 stt:4,0 qh:6 cast:4,0 mm2:5,0 stt:4,1 cast:4,1 mm2:5,1
+tr:4,0 sty:4,0 stt:4,2 cast:4,2 stt:4,3 cast:4,3 sty:4,1 qy:3 gain:7 tr:4,1 mm2:5,2 mm2:5,3 wc:4,0
+wc:4,1 stt:5,0 qh:7 cast:5,0 mm2:6,0 stt:5,1 cast:5,1 mm2:6,1 tr:5,0 sty:5,0 stt:5,2 cast:5,2
+stt:5,3 cast:5,3 sty:5,1 qy:4 tr:5,1 mm2:6,2 mm2:6,3 wc:5,0 wc:5,1 stt:6,0 mm2:7,0 cast:6,0 stt:6,1
+mm2:7,1 cast:6,1 sty:6,0 stt:6,2 mm2:7,2 cast:6,2 stt:6,3 mm2:7,3 tr:6,0 cast:6,3 sty:6,1 qy:5
+ss:0,1536 tr:6,1 stt:7,0 wc:6,0 stt:7,1 sty:7,0 cast:7,0 stt:7,2 cast:7,1 tr:7,0 stt:7,3 sty:7,1
+wcv:6,1 cast:7,2 castv:7,3 tr:7,1 qy:6 wc:7,0 qyh:7,0 wcv:7,1 qyh:7,1 sse:1536,2048
 """
 
 
@@ -55,7 +55,8 @@ def tile_noise_level_bias_table_k7_kernel(
         ident = keep.tile([P, P], F32)
         vec_rows = keep.tile([P, 512], BF16)
         vec = keep.tile([P, 2 * HALVES, 4], F32)
-        fade_col = keep.tile([P, 4, 2], BF16)
+        row_words = keep.tile([P, P], F32)
+        col_words = keep.tile([P, 32], F32)
         warm = keep.tile([P, 8], F32)
         feats_rows = keep.tile([P, 4, K], BF16)
         feats_k = keep.tile([P, T, 2], F32, align_bytes=64)
@@ -63,13 +64,13 @@ def tile_noise_level_bias_table_k7_kernel(
         feats_s = keep.tile([P, T], U8, align_bytes=64)
         w1_raw0 = keep.tile([P, 1, 2 * F], U8, align_bytes=64)
         w1_raw = keep.tile([P, G - 1, 2 * F], U8, align_bytes=64)
-        w1s_raw0 = keep.tile([P, 1, F], U8, align_bytes=64)
-        w1s_raw = keep.tile([P, G - 1, F], U8, align_bytes=64)
+        w1s_raw = keep.tile([P, F], U8, align_bytes=64)
+        w1s_packed = keep.tile([P, F], U8, align_bytes=64)
         w1_q = keep.tile([P, HALVES, 1024], U8, align_bytes=64)
-        w1_s = keep.tile([P, G, F], U8, align_bytes=64)
+        w1_s = keep.tile([P, G - 1, F], U8, align_bytes=64)
         w2_q = keep.tile([P, HALVES, 2 * D], U8, align_bytes=64)
         w2_s = keep.tile([P, HALVES, D], U8, align_bytes=64)
-        table_all = keep.tile([P, G, D], BF16)
+        table_all = keep.tile([P, G, D // 2], F32)
         y_s = keep.tile([P, 2, G * T], U8, align_bytes=64)
 
         def load_scale_rows(queue, plane, rows):
@@ -80,51 +81,54 @@ def tile_noise_level_bias_table_k7_kernel(
                 )
 
         nc.vector.memset(vec_rows[:], 0.0)
-        nc.vector.memset(w1s_raw0[:].bitcast(I32), 0)
-        nc.vector.memset(warm[:], 0.0)
         nc.vector.memset(w1s_raw[:].bitcast(I32), 0)
+        nc.vector.memset(warm[:], 0.0)
+        nc.vector.memset(row_words[:], 0.0)
+        nc.vector.memset(w1_s[:].bitcast(I32), 0)
         nc.vector.memset(w2_s[:].bitcast(I32), 0)
         make_identity(nc, ident[:])
 
-        nc.sync.dma_start(out=vec_rows[0:HALVES, :], in_=b1.rearrange("b (g c) -> (b g) c", g=2))
-        nc.scalar.dma_start(
-            out=vec_rows[HALVES : 2 * HALVES, :], in_=gain.rearrange("b (g c) -> (b g) c", g=2)
+        nc.sync.dma_start(
+            out=feats_rows[:].rearrange("q (h j) k -> q h (j k)", j=2),
+            in_=feats.rearrange("(h q j) k -> q h (j k)", q=P, j=2),
         )
-        nc.sync.dma_start(out=feats_rows[:], in_=feats.rearrange("(i q) k -> q i k", q=P))
         nc.sync.dma_start(
             out=w1_raw0[:].bitcast(I32), in_=w1_words[0:1].rearrange("g p n -> p g n").bitcast(I32)
         )
-        load_scale_rows(nc.scalar, w1s_raw0, w1_scales[0:1])
+        nc.scalar.dma_start(out=vec_rows[0:HALVES, :], in_=b1.rearrange("b (g c) -> (b g) c", g=2))
+        nc.scalar.dma_start(
+            out=vec_rows[HALVES : 2 * HALVES, :], in_=gain.rearrange("b (g c) -> (b g) c", g=2)
+        )
+        for quad in range(4):
+            nc.scalar.dma_start(
+                out=w1s_raw[32 * quad : 32 * quad + 16, :].bitcast(I32),
+                in_=w1_scales[:, 4 * quad : 4 * quad + 4, :].bitcast(I32),
+            )
         nc.scalar.activation(out=warm[:, 4:5], in_=warm[:, 0:1], func=ACT.Silu)
-        load_scale_rows(nc.sync, w1s_raw, w1_scales[1:G])
         nc.sync.dma_start(
             out=w1_raw[:].bitcast(I32), in_=w1_words[1:G].rearrange("g p n -> p g n").bitcast(I32)
         )
-        load_scale_rows(nc.sync, w2_s, w2_scales)
-        with nc.allow_non_contiguous_dma(reason="one fade value a partition"):
-            nc.sync.dma_start(
-                out=fade_col[:, :, 0:1], in_=fade.rearrange("(i q o) -> q i o", q=P, o=1)
-            )
-        for b in range(G):
-            nc.sync.dma_start(
-                out=w2_q[:, 2 * b : 2 * b + 2, :].bitcast(I32),
-                in_=w2_words[2 * b : 2 * b + 2].rearrange("g p n -> p g n").bitcast(I32),
-            )
-            nc.sync.dma_start(out=table_all[:, b, :], in_=table[b].partition_broadcast(P))
+        row_values = row_words[:].bitcast(BF16)
+        nc.sync.dma_start(out=row_values[0:16, :], in_=table.rearrange("b (m c) -> (b m) c", c=256))
+        nc.sync.dma_start(out=row_values[16:18, :], in_=fade.rearrange("(h c) -> h c", c=256))
+
+        def later_loads():
+            for b in range(1, G):
+                for quad in range(4):
+                    nc.sync.dma_start(
+                        out=w1_s[32 * quad : 32 * quad + 4, b - 1, :].bitcast(I32),
+                        in_=w1s_packed[32 * quad + 4 * b : 32 * quad + 4 * b + 4, :].bitcast(I32),
+                    )
+            load_scale_rows(nc.sync, w2_s[:, 0:4, :], w2_scales[0:4])
+            load_scale_rows(nc.sync, w2_s[:, 4:8, :], w2_scales[4:8])
+            for b in range(G):
+                nc.sync.dma_start(
+                    out=w2_q[:, 2 * b : 2 * b + 2, :].bitcast(I32),
+                    in_=w2_words[2 * b : 2 * b + 2].rearrange("g p n -> p g n").bitcast(I32),
+                )
 
         def turn_words(bank, slot, words):
             nc.tensor.transpose(bank[:, slot * P : (slot + 1) * P], words, ident[:])
-
-        vec_bank = psum.tile([P, 512], F32, tag="z", name="vec_bank")
-        vec_words = vec_rows[:].bitcast(F32)
-        for u in range(2):
-            turn_words(vec_bank, u, vec_words[:, u:256:2])
-        nc.scalar.copy(
-            out=vec[:].rearrange("p r (u e) -> p r u e", e=2),
-            in_=vec_bank[:, 0 : 2 * P].bitcast(BF16).rearrange("p (u r e) -> p r u e", u=2, e=2)[
-                :, 0 : 2 * HALVES
-            ],
-        )
 
         def order_w1_words(half):
             b, g = divmod(half, 2)
@@ -134,12 +138,27 @@ def tile_noise_level_bias_table_k7_kernel(
                 in_=raw[:, 1024 * g : 1024 * (g + 1)].rearrange("p (m t e) -> p t m e", t=4, e=2),
             )
 
-        def order_w1_scales(b):
-            raw = w1s_raw0[:, 0, :] if b == 0 else w1s_raw[:, b - 1, :]
+        def order_w1_scales():
             nc.vector.tensor_copy(
-                out=w1_s[:, b, :].rearrange("p (g t m) -> p g t m", g=2, t=4),
-                in_=raw.rearrange("p (g m t) -> p g t m", g=2, t=4),
+                out=w1s_packed[:].rearrange("p (g t m) -> p g t m", g=2, t=4),
+                in_=w1s_raw[:].rearrange("p (g m t) -> p g t m", g=2, t=4),
             )
+
+        def turn_rows():
+            bank = psum.tile([P, 512], F32, tag="t", name="rows_bank")
+            turn_words(bank, 0, row_words[:])
+            nc.scalar.copy(out=col_words[:], in_=bank[:, 0:32])
+
+        table_banks = {}
+
+        def spread_table(b):
+            bank = psum.tile([P, 512], F32, tag="t", name="table_bank")
+            for m in range(4):
+                turn_words(bank, m, col_words[:, 4 * b + m : 4 * b + m + 1].to_broadcast([P, P]))
+            table_banks[b] = bank
+
+        def keep_table(b):
+            nc.scalar.copy(out=table_all[:, b, :], in_=table_banks[b][:])
 
         feats_words = feats_rows[:].bitcast(F32)
         feats_banks = []
@@ -154,21 +173,29 @@ def tile_noise_level_bias_table_k7_kernel(
                 out=feats_k[:, 256 * pair : 256 * (pair + 1), :].rearrange("p (j q) u -> p j q u", j=2),
                 in_=feats_banks[pair][:].rearrange("p (j u q) -> p j q u", j=2, u=2),
             )
-        order_w1_scales(0)
+        vec_bank = psum.tile([P, 512], F32, tag="z", name="vec_bank")
+        vec_words = vec_rows[:].bitcast(F32)
+        for u in range(2):
+            turn_words(vec_bank, u, vec_words[:, u:256:2])
+        nc.scalar.copy(
+            out=vec[:].rearrange("p r (u e) -> p r u e", e=2),
+            in_=vec_bank[:, 0 : 2 * P].bitcast(BF16).rearrange("p (u r e) -> p r u e", u=2, e=2)[
+                :, 0 : 2 * HALVES
+            ],
+        )
+
         order_w1_words(0)
+        order_w1_scales()
+        later_loads()
         order_w1_words(1)
-        order_w1_scales(1)
         order_w1_words(2)
-        order_w1_words(3)
         nc.vector.quantize_mx(
             out=feats_q[:].bitcast(FP8X4),
             scales=feats_s[:],
             in_=feats_k[:].rearrange("p n u -> p (n u)").bitcast(BF16),
         )
-        order_w1_scales(2)
-        order_w1_words(4)
-        order_w1_words(5)
-        order_w1_scales(3)
+        for half in range(3, 6):
+            order_w1_words(half)
 
         z_banks, silu_tiles, h_tiles, h_q, h_s = {}, {}, {}, {}, {}
         p_banks, y_tiles, yb_tiles, t_banks, yk_tiles = {}, {}, {}, {}, {}
@@ -179,7 +206,7 @@ def tile_noise_level_bias_table_k7_kernel(
             nc.tensor.matmul_mx(
                 out=bank[:],
                 lhsT=w1_q[:, half, 256 * t : 256 * (t + 1)].bitcast(FP4X4),
-                lhsT_scale=w1_s[:, b, 512 * g + P * t : 512 * g + P * (t + 1)],
+                lhsT_scale=(w1s_packed[:] if b == 0 else w1_s[:, b - 1, :])[:, 512 * g + P * t : 512 * g + P * (t + 1)],
                 rhs=feats_q[:].bitcast(FP8X4),
                 rhs_scale=feats_s[:],
                 start=True,
@@ -233,8 +260,8 @@ def tile_noise_level_bias_table_k7_kernel(
             nc.vector.scalar_tensor_tensor(
                 out=y_tiles[half, pair][:, j, :],
                 in0=p_banks[half, i][:],
-                scalar=fade_col[:, i, 0:1],
-                in1=table_all[:, b, 512 * g : 512 * (g + 1)],
+                scalar=col_words[:].bitcast(BF16)[:, 32 + i : 33 + i],
+                in1=table_all[:, b, :].bitcast(BF16)[:, 512 * g : 512 * (g + 1)],
                 op0=ALU.mult,
                 op1=ALU.add,
             )
@@ -243,7 +270,7 @@ def tile_noise_level_bias_table_k7_kernel(
             b, g = divmod(half, 2)
             nc.sync.dma_start(
                 out=out_0[b, 256 * pair : 256 * (pair + 1), 512 * g : 512 * (g + 1)].rearrange(
-                    "(j q) c -> q j c", q=P
+                    "(q j) c -> q j c", q=P
                 ),
                 in_=y_tiles[half, pair][:],
             )
@@ -266,11 +293,12 @@ def tile_noise_level_bias_table_k7_kernel(
             t_banks[half, first] = bank
 
         def gather_y(half, first, count, engine_copy):
+            pair, j = divmod(first, 2)
             if half not in yk_tiles:
                 yk_tiles[half] = work.tile([P, T, 2], F32, tag="yk", name="yk_tile", align_bytes=64)
             engine_copy(
-                out=yk_tiles[half][:, P * first : P * (first + count), :].rearrange("p (j q) u -> p j q u", j=count),
-                in_=t_banks[half, first][:, 0 : 2 * P * count].rearrange("p (j u q) -> p j q u", j=count, u=2),
+                out=yk_tiles[half][:, 256 * pair : 256 * (pair + 1), :].rearrange("p (q j) u -> p q j u", j=2),
+                in_=t_banks[half, first][:].rearrange("p (j u q) -> p q j u", j=2, u=2),
             )
 
         def quantize_y(half, first, count):
@@ -297,6 +325,9 @@ def tile_noise_level_bias_table_k7_kernel(
         on_scalar, on_vector = nc.scalar.copy, nc.vector.tensor_copy
         calls = {
             "mm1": first_matmul,
+            "rows": lambda unused: turn_rows(),
+            "tb": spread_table,
+            "tc": keep_table,
             "silu": silu,
             "gain": apply_gain,
             "qh": quantize_h,

from contextlib import ExitStack

import concourse.mybir as mybir
from concourse.masks import make_identity

G, T, K, F, D = 4, 512, 512, 1024, 1024
FLOPS = 2 * G * T * (K * F + F * D)

F32 = mybir.dt.float32
BF16 = mybir.dt.bfloat16
I32 = mybir.dt.int32
U32 = mybir.dt.uint32
U8 = mybir.dt.uint8
FP8X4 = mybir.dt.float8_e4m3fn_x4
FP4X4 = mybir.dt.float4_e2m1fn_x4
ACT = mybir.ActivationFunctionType
ALU = mybir.AluOpType

P = 128
HALVES = 2 * G
SILU_LEAD = 3
ORDER = """mm1:0,0 silu:0,0 mm1:0,1 silu:0,1 mm1:0,2 silu:0,2 mm1:0,3 silu:0,3 mm1:1,0 mm1:1,1 gain:0 silu:1,0
mm1:1,2 silu:1,1 mm1:1,3 rows:0 silu:1,2 mm1:2,0 silu:1,3 mm1:2,1 tb:0 pc:6 qh:0 gain:1 silu:2,0
mm1:2,2 silu:2,1 mm1:2,3 tc:0 tb:1 silu:2,2 mm1:3,0 silu:2,3 mm1:3,1 tc:1 tb:2 tb:3 pc:7 qh:1
mm2:0,0 mm2:0,1 gain:2 silu:3,0 mm1:3,2 silu:3,1 tc:2 tc:3 mm1:3,3 mm2:0,2 mm2:0,3 silu:3,2 mm1:4,0
silu:3,3 mm1:4,1 stt:0,0 qh:2 cast:0,0 mm2:1,0 stt:0,1 cast:0,1 mm2:1,1 tr:0,0 sty:0,0 stt:0,2
cast:0,2 stt:0,3 cast:0,3 sty:0,1 gain:3 silu:4,0 tr:0,1 mm1:4,2 silu:4,1 mm1:4,3 mm2:1,2 mm2:1,3
wc:0,0 silu:4,2 mm1:5,0 wc:0,1 silu:4,3 mm1:5,1 stt:1,0 qh:3 cast:1,0 mm2:2,0 stt:1,1 cast:1,1
mm2:2,1 tr:1,0 sty:1,0 stt:1,2 cast:1,2 stt:1,3 cast:1,3 sty:1,1 qy:0 gain:4 silu:5,0 tr:1,1 mm1:5,2
silu:5,1 mm1:5,3 mm2:2,2 mm2:2,3 wc:1,0 silu:5,2 mm1:6,0 wc:1,1 silu:5,3 mm1:6,1 stt:2,0 qh:4
cast:2,0 mm2:3,0 stt:2,1 cast:2,1 mm2:3,1 tr:2,0 sty:2,0 stt:2,2 cast:2,2 stt:2,3 cast:2,3 sty:2,1
qy:1 gain:5 silu:6,0 tr:2,1 mm1:6,2 silu:6,1 mm1:6,3 mm2:3,2 mm2:3,3 wc:2,0 silu:6,2 mm1:7,0 wc:2,1
silu:6,3 mm1:7,1 stt:3,0 qh:5 cast:3,0 mm2:4,0 stt:3,1 cast:3,1 mm2:4,1 tr:3,0 sty:3,0 stt:3,2
cast:3,2 stt:3,3 cast:3,3 sty:3,1 qy:2 gain:6 silu:7,0 tr:3,1 mm1:7,2 silu:7,1 mm1:7,3 mm2:4,2
mm2:4,3 wc:3,0 silu:7,2 wc:3,1 silu:7,3 stt:4,0 qh:6 cast:4,0 mm2:5,0 stt:4,1 cast:4,1 mm2:5,1
tr:4,0 sty:4,0 stt:4,2 cast:4,2 stt:4,3 cast:4,3 sty:4,1 qy:3 gain:7 tr:4,1 mm2:5,2 mm2:5,3 wc:4,0
wc:4,1 stt:5,0 qh:7 cast:5,0 mm2:6,0 stt:5,1 cast:5,1 mm2:6,1 tr:5,0 sty:5,0 stt:5,2 cast:5,2
stt:5,3 cast:5,3 sty:5,1 qy:4 tr:5,1 mm2:6,2 mm2:6,3 wc:5,0 wc:5,1 stt:6,0 mm2:7,0 cast:6,0 stt:6,1
mm2:7,1 cast:6,1 sty:6,0 stt:6,2 mm2:7,2 cast:6,2 stt:6,3 mm2:7,3 tr:6,0 cast:6,3 sty:6,1 qy:5
ss:0,1536 tr:6,1 stt:7,0 wc:6,0 stt:7,1 sty:7,0 cast:7,0 stt:7,2 cast:7,1 tr:7,0 stt:7,3 sty:7,1
wcv:6,1 cast:7,2 castv:7,3 tr:7,1 qy:6 wc:7,0 qyh:7,0 wcv:7,1 qyh:7,1 sse:1536,2048
"""


def tile_noise_level_bias_table_k7_kernel(
    tc, feats, w1_words, w1_scales, b1, gain, w2_words, w2_scales, fade, table, out_0, out_1, out_2
):
    nc = tc.nc
    with ExitStack() as ctx:
        keep = ctx.enter_context(tc.tile_pool(name="keep", bufs=1))
        work = ctx.enter_context(tc.tile_pool(name="work", bufs=2))
        psum = ctx.enter_context(tc.psum_pool(name="psum", bufs=2))
        ctx.enter_context(tc.manual_schedule())

        ident = keep.tile([P, P], F32)
        vec_rows = keep.tile([P, 512], BF16)
        vec = keep.tile([P, 2 * HALVES, 4], F32)
        row_words = keep.tile([P, P], F32)
        col_words = keep.tile([P, 32], F32)
        warm = keep.tile([P, 8], F32)
        feats_rows = keep.tile([P, 4, K], BF16)
        feats_k = keep.tile([P, T, 2], F32, align_bytes=64)
        feats_q = keep.tile([P, T], U32, align_bytes=64)
        feats_s = keep.tile([P, T], U8, align_bytes=64)
        w1_raw0 = keep.tile([P, 1, 2 * F], U8, align_bytes=64)
        w1_raw = keep.tile([P, G - 1, 2 * F], U8, align_bytes=64)
        w1s_raw = keep.tile([P, F], U8, align_bytes=64)
        w1s_packed = keep.tile([P, F], U8, align_bytes=64)
        w1_q = keep.tile([P, HALVES, 1024], U8, align_bytes=64)
        w1_s = keep.tile([P, G - 1, F], U8, align_bytes=64)
        w2_q = keep.tile([P, HALVES, 2 * D], U8, align_bytes=64)
        w2_s = keep.tile([P, HALVES, D], U8, align_bytes=64)
        table_all = keep.tile([P, G, D // 2], F32)
        y_s = keep.tile([P, 2, G * T], U8, align_bytes=64)

        def load_scale_rows(queue, plane, rows):
            for quad in range(4):
                queue.dma_start(
                    out=plane[32 * quad : 32 * quad + 4].bitcast(I32),
                    in_=rows[:, 4 * quad : 4 * quad + 4, :].rearrange("g r n -> r g n").bitcast(I32),
                )

        nc.vector.memset(vec_rows[:], 0.0)
        nc.vector.memset(w1s_raw[:].bitcast(I32), 0)
        nc.vector.memset(warm[:], 0.0)
        nc.vector.memset(row_words[:], 0.0)
        nc.vector.memset(w1_s[:].bitcast(I32), 0)
        nc.vector.memset(w2_s[:].bitcast(I32), 0)
        make_identity(nc, ident[:])

        nc.sync.dma_start(
            out=feats_rows[:].rearrange("q (h j) k -> q h (j k)", j=2),
            in_=feats.rearrange("(h q j) k -> q h (j k)", q=P, j=2),
        )
        nc.sync.dma_start(
            out=w1_raw0[:].bitcast(I32), in_=w1_words[0:1].rearrange("g p n -> p g n").bitcast(I32)
        )
        nc.scalar.dma_start(out=vec_rows[0:HALVES, :], in_=b1.rearrange("b (g c) -> (b g) c", g=2))
        nc.scalar.dma_start(
            out=vec_rows[HALVES : 2 * HALVES, :], in_=gain.rearrange("b (g c) -> (b g) c", g=2)
        )
        for quad in range(4):
            nc.scalar.dma_start(
                out=w1s_raw[32 * quad : 32 * quad + 16, :].bitcast(I32),
                in_=w1_scales[:, 4 * quad : 4 * quad + 4, :].bitcast(I32),
            )
        nc.scalar.activation(out=warm[:, 4:5], in_=warm[:, 0:1], func=ACT.Silu)
        nc.sync.dma_start(
            out=w1_raw[:].bitcast(I32), in_=w1_words[1:G].rearrange("g p n -> p g n").bitcast(I32)
        )
        row_values = row_words[:].bitcast(BF16)
        nc.sync.dma_start(out=row_values[0:16, :], in_=table.rearrange("b (m c) -> (b m) c", c=256))
        nc.sync.dma_start(out=row_values[16:18, :], in_=fade.rearrange("(h c) -> h c", c=256))

        def later_loads():
            for b in range(1, G):
                for quad in range(4):
                    nc.sync.dma_start(
                        out=w1_s[32 * quad : 32 * quad + 4, b - 1, :].bitcast(I32),
                        in_=w1s_packed[32 * quad + 4 * b : 32 * quad + 4 * b + 4, :].bitcast(I32),
                    )
            load_scale_rows(nc.sync, w2_s[:, 0:4, :], w2_scales[0:4])
            load_scale_rows(nc.sync, w2_s[:, 4:8, :], w2_scales[4:8])
            for b in range(G):
                nc.sync.dma_start(
                    out=w2_q[:, 2 * b : 2 * b + 2, :].bitcast(I32),
                    in_=w2_words[2 * b : 2 * b + 2].rearrange("g p n -> p g n").bitcast(I32),
                )

        def turn_words(bank, slot, words):
            nc.tensor.transpose(bank[:, slot * P : (slot + 1) * P], words, ident[:])

        def order_w1_words(half):
            b, g = divmod(half, 2)
            raw = w1_raw0[:, 0, :] if b == 0 else w1_raw[:, b - 1, :]
            nc.vector.tensor_copy(
                out=w1_q[:, half, :].rearrange("p (t m e) -> p t m e", t=4, e=2),
                in_=raw[:, 1024 * g : 1024 * (g + 1)].rearrange("p (m t e) -> p t m e", t=4, e=2),
            )

        def order_w1_scales():
            nc.vector.tensor_copy(
                out=w1s_packed[:].rearrange("p (g t m) -> p g t m", g=2, t=4),
                in_=w1s_raw[:].rearrange("p (g m t) -> p g t m", g=2, t=4),
            )

        def turn_rows():
            bank = psum.tile([P, 512], F32, tag="t", name="rows_bank")
            turn_words(bank, 0, row_words[:])
            nc.scalar.copy(out=col_words[:], in_=bank[:, 0:32])

        table_banks = {}

        def spread_table(b):
            bank = psum.tile([P, 512], F32, tag="t", name="table_bank")
            for m in range(4):
                turn_words(bank, m, col_words[:, 4 * b + m : 4 * b + m + 1].to_broadcast([P, P]))
            table_banks[b] = bank

        def keep_table(b):
            nc.scalar.copy(out=table_all[:, b, :], in_=table_banks[b][:])

        feats_words = feats_rows[:].bitcast(F32)
        feats_banks = []
        for pair in range(2):
            bank = psum.tile([P, 512], F32, tag="t", name="feats_bank")
            for j in range(2):
                for u in range(2):
                    turn_words(bank, 2 * j + u, feats_words[:, 2 * pair + j, u:256:2])
            feats_banks.append(bank)
        for pair in range(2):
            nc.scalar.copy(
                out=feats_k[:, 256 * pair : 256 * (pair + 1), :].rearrange("p (j q) u -> p j q u", j=2),
                in_=feats_banks[pair][:].rearrange("p (j u q) -> p j q u", j=2, u=2),
            )
        vec_bank = psum.tile([P, 512], F32, tag="z", name="vec_bank")
        vec_words = vec_rows[:].bitcast(F32)
        for u in range(2):
            turn_words(vec_bank, u, vec_words[:, u:256:2])
        nc.scalar.copy(
            out=vec[:].rearrange("p r (u e) -> p r u e", e=2),
            in_=vec_bank[:, 0 : 2 * P].bitcast(BF16).rearrange("p (u r e) -> p r u e", u=2, e=2)[
                :, 0 : 2 * HALVES
            ],
        )

        order_w1_words(0)
        order_w1_scales()
        later_loads()
        order_w1_words(1)
        order_w1_words(2)
        nc.vector.quantize_mx(
            out=feats_q[:].bitcast(FP8X4),
            scales=feats_s[:],
            in_=feats_k[:].rearrange("p n u -> p (n u)").bitcast(BF16),
        )
        for half in range(3, 6):
            order_w1_words(half)

        z_banks, silu_tiles, h_tiles, h_q, h_s = {}, {}, {}, {}, {}
        p_banks, y_tiles, yb_tiles, t_banks, yk_tiles = {}, {}, {}, {}, {}

        def first_matmul(half, t):
            b, g = divmod(half, 2)
            bank = psum.tile([P, T], F32, tag="z", name="z_bank")
            nc.tensor.matmul_mx(
                out=bank[:],
                lhsT=w1_q[:, half, 256 * t : 256 * (t + 1)].bitcast(FP4X4),
                lhsT_scale=(w1s_packed[:] if b == 0 else w1_s[:, b - 1, :])[:, 512 * g + P * t : 512 * g + P * (t + 1)],
                rhs=feats_q[:].bitcast(FP8X4),
                rhs_scale=feats_s[:],
                start=True,
                stop=True,
            )
            z_banks[half, t] = bank

        def silu(half, t):
            if t == 0:
                silu_tiles[half] = work.tile([P, 4, T], F32, tag="silu", name="silu_tile", bufs=SILU_LEAD + 1)
            nc.scalar.activation(
                out=silu_tiles[half][:, t, :], in_=z_banks[half, t][:], func=ACT.Silu, bias=vec[:, half, t : t + 1]
            )

        def apply_gain(half):
            h = work.tile([P, 4 * T], BF16, tag="h", name="h_tile", align_bytes=64)
            nc.vector.tensor_tensor(
                out=h[:].rearrange("p (j e t) -> p j t e", e=2, t=4),
                in0=silu_tiles[half][:].rearrange("p t (j e) -> p j t e", e=2),
                in1=vec[:, HALVES + half, :].unsqueeze(1).unsqueeze(3).to_broadcast([P, T // 2, 4, 2]),
                op=ALU.mult,
            )
            h_tiles[half] = h

        def quantize_h(half):
            codes = work.tile([P, T], U32, tag="hq", name="h_codes", bufs=4, align_bytes=64)
            scales = work.tile([P, T], U8, tag="hs", name="h_scales", bufs=4, align_bytes=64)
            nc.vector.quantize_mx(out=codes[:].bitcast(FP8X4), scales=scales[:], in_=h_tiles[half][:])
            h_q[half], h_s[half] = codes, scales

        def second_matmul(half, i):
            b, g = divmod(half, 2)
            bank = psum.tile([P, 512], F32, tag="p", name="p_bank", bufs=4)
            for kp in range(2):
                nc.tensor.matmul_mx(
                    out=bank[:],
                    lhsT=h_q[2 * b + kp][:, P * i : P * (i + 1)].bitcast(FP8X4),
                    lhsT_scale=h_s[2 * b + kp][:, P * i : P * (i + 1)],
                    rhs=w2_q[:, 2 * b + kp, 1024 * g : 1024 * (g + 1)].bitcast(FP4X4),
                    rhs_scale=w2_s[:, 2 * b + kp, 512 * g : 512 * (g + 1)],
                    start=(kp == 0),
                    stop=(kp == 1),
                )
            p_banks[half, i] = bank

        def fade_and_table(half, i):
            b, g = divmod(half, 2)
            pair, j = divmod(i, 2)
            if j == 0:
                y_tiles[half, pair] = work.tile([P, 2, 512], F32, tag="y", name="y_tile", bufs=5)
            nc.vector.scalar_tensor_tensor(
                out=y_tiles[half, pair][:, j, :],
                in0=p_banks[half, i][:],
                scalar=col_words[:].bitcast(BF16)[:, 32 + i : 33 + i],
                in1=table_all[:, b, :].bitcast(BF16)[:, 512 * g : 512 * (g + 1)],
                op0=ALU.mult,
                op1=ALU.add,
            )

        def store_y(half, pair):
            b, g = divmod(half, 2)
            nc.sync.dma_start(
                out=out_0[b, 256 * pair : 256 * (pair + 1), 512 * g : 512 * (g + 1)].rearrange(
                    "(q j) c -> q j c", q=P
                ),
                in_=y_tiles[half, pair][:],
            )

        def round_y(half, i, engine_copy):
            pair, j = divmod(i, 2)
            if j == 0:
                yb_tiles[half, pair] = work.tile([P, 2, 512], BF16, tag="yb", name="yb_tile", bufs=4)
            engine_copy(
                out=yb_tiles[half, pair][:, j, :].rearrange("q (u p e) -> q u p e", u=2, e=2),
                in_=y_tiles[half, pair][:, j, :].rearrange("q (p u e) -> q u p e", u=2, e=2),
            )

        def turn_y(half, first, count, tag="t", bufs=2):
            bank = psum.tile([P, 512], F32, tag=tag, name="y_bank", bufs=bufs)
            pair, j = divmod(first, 2)
            words = yb_tiles[half, pair][:].rearrange("q j c -> q (j c)").bitcast(F32)
            for slot in range(2 * count):
                turn_words(bank, slot, words[:, P * (2 * j + slot) : P * (2 * j + slot + 1)])
            t_banks[half, first] = bank

        def gather_y(half, first, count, engine_copy):
            pair, j = divmod(first, 2)
            if half not in yk_tiles:
                yk_tiles[half] = work.tile([P, T, 2], F32, tag="yk", name="yk_tile", align_bytes=64)
            engine_copy(
                out=yk_tiles[half][:, 256 * pair : 256 * (pair + 1), :].rearrange("p (q j) u -> p q j u", j=2),
                in_=t_banks[half, first][:].rearrange("p (j u q) -> p q j u", j=2, u=2),
            )

        def quantize_y(half, first, count):
            b, g = divmod(half, 2)
            cols = slice(T * b + P * first, T * b + P * (first + count))
            codes = work.tile([P, P * count], U32, tag="yq", name="y_codes", bufs=3, align_bytes=64)
            nc.vector.quantize_mx(
                out=codes[:].bitcast(FP8X4),
                scales=y_s[:, g, cols],
                in_=yk_tiles[half][:, P * first : P * (first + count), :].rearrange("p n u -> p (n u)").bitcast(BF16),
            )
            nc.sync.dma_start(
                out=out_1[g].rearrange("p m t -> p (m t)")[:, 4 * cols.start : 4 * cols.stop].bitcast(I32),
                in_=codes[:].bitcast(I32),
            )

        def store_y_scales(first, last, queues):
            for quad in range(4):
                queues[quad % len(queues)].dma_start(
                    out=out_2[:, 4 * quad : 4 * quad + 4, first:last].rearrange("g r m -> r g m").bitcast(I32),
                    in_=y_s[32 * quad : 32 * quad + 4, :, first:last].bitcast(I32),
                )

        on_scalar, on_vector = nc.scalar.copy, nc.vector.tensor_copy
        calls = {
            "mm1": first_matmul,
            "rows": lambda unused: turn_rows(),
            "tb": spread_table,
            "tc": keep_table,
            "silu": silu,
            "gain": apply_gain,
            "qh": quantize_h,
            "pc": order_w1_words,
            "mm2": second_matmul,
            "stt": fade_and_table,
            "sty": store_y,
            "cast": lambda half, i: round_y(half, i, on_scalar),
            "castv": lambda half, i: round_y(half, i, on_vector),
            "tr": lambda half, pair: turn_y(half, 2 * pair, 2),
            "tri": lambda half, i: turn_y(half, i, 1, "z", 2),
            "wc": lambda half, pair: gather_y(half, 2 * pair, 2, on_scalar),
            "wcv": lambda half, pair: gather_y(half, 2 * pair, 2, on_vector),
            "wci": lambda half, i: gather_y(half, i, 1, on_scalar),
            "wciv": lambda half, i: gather_y(half, i, 1, on_vector),
            "qy": lambda half: quantize_y(half, 0, 4),
            "qyh": lambda half, pair: quantize_y(half, 2 * pair, 2),
            "ss": lambda first, last: store_y_scales(first, last, [nc.sync]),
            "sse": lambda first, last: store_y_scales(first, last, [nc.scalar, nc.sync]),
        }
        for item in ORDER.split():
            call, args = item.split(":")
            calls[call](*[int(a) for a in args.split(",")])
